import numpy as np
CORES = [5,13,21,29,37,45,53,61,197,205,213,221,229,237,245,253]
N = 16
T = 256
ROUTE = [[[7,6],[0,1],[4,2],[5,9],[3,11],[0,10],[4,12],[6,3],[7,1],[15,4],[12,9],[10,11],[9,3],[5,3],[2,11],[1,10],[15,4],[10,13],[4,6],[4,0],[4,2],[15,1],[3,4],[13,15],[13,11],[13,11],[13,2],[14,10],[3,6],[4,6],[14,6],[10,7],[11,12],[15,8],[4,11],[13,10],[1,5],[2,8],[3,11],[0,13],[1,8],[14,6],[10,14],[4,15],[7,4],[11,13],[9,11],[2,13],[10,2],[12,4],[7,11],[6,0],[1,13],[0,1],[4,14],[2,11],[10,4],[3,0],[8,14],[3,11],[14,10],[1,9],[12,11],[5,2],[14,4],[6,15],[3,14],[8,12],[0,1],[4,9],[7,1],[10,3],[11,2],[4,10],[12,3],[12,2],[14,2],[9,1],[14,3],[14,4],[11,2],[1,9],[12,8],[1,2],[1,10],[6,12],[0,13],[5,7],[0,13],[2,8],[1,13],[0,7],[13,6],[8,11],[11,12],[14,6],[9,7],[11,13],[3,0],[13,3],[11,5],[4,9],[1,6],[7,11],[13,1],[1,5],[12,13],[8,14],[12,14],[0,1],[7,3],[13,2],[1,4],[3,15],[8,6],[0,12],[15,6],[11,6],[1,5],[14,12],[4,2],[1,9],[5,4],[0,8],[4,9],[3,0],[10,5],[3,7],[11,14],[10,0],[11,6],[10,13],[4,7],[10,14],[13,15],[3,0],[4,0],[2,0],[6,5],[1,10],[5,8],[1,11],[3,8],[6,7],[5,4],[10,12],[11,15],[11,13],[12,5],[3,14],[9,3],[15,1],[6,1],[5,9],[7,10],[7,5],[9,10],[11,15],[14,5],[15,10],[11,15],[15,5],[15,14],[10,13],[0,3],[3,9],[12,9],[0,5],[13,9],[9,11],[1,2],[9,10],[7,3],[7,10],[0,11],[10,7],[4,12],[0,1],[9,1],[0,11],[3,14],[14,10],[15,8],[15,2],[8,10],[10,1],[0,1],[9,6],[15,10],[12,5],[8,4],[15,0],[6,2],[4,10],[11,10],[14,8],[1,5],[8,1],[8,3],[4,7],[13,15],[0,12],[9,11],[13,3],[11,15],[7,6],[8,7],[3,10],[11,6],[6,14],[11,1],[7,3],[2,0],[14,9],[2,13],[7,10],[5,6],[1,5],[1,12],[7,14],[5,7],[11,9],[5,12],[12,2],[13,9],[13,4],[6,8],[9,12],[1,11],[2,4],[11,9],[12,6],[11,14],[8,0],[15,9],[13,11],[8,12],[15,4],[15,8],[1,15],[8,14],[12,8],[2,1],[1,8],[2,11],[14,3],[8,12],[12,13],[0,5],[1,2],[3,6],[0,12],[5,1],[3,14],[9,12],[2,4]],[[11,15],[9,1],[6,8],[14,4],[3,14],[12,0],[1,2],[14,13],[1,0],[4,11],[11,7],[15,14],[0,14],[10,15],[1,0],[10,5],[8,13],[9,5],[11,10],[13,4],[12,15],[11,15],[0,15],[1,11],[15,12],[2,13],[3,1],[5,12],[8,14],[2,14],[11,1],[2,1],[3,2],[12,6],[15,0],[5,8],[6,3],[1,10],[5,3],[6,4],[14,10],[0,6],[3,7],[0,4],[1,3],[5,13],[15,4],[4,2],[11,4],[0,1],[6,10],[2,13],[3,13],[4,11],[0,5],[3,6],[15,14],[10,14],[5,14],[8,12],[10,7],[6,4],[5,11],[8,9],[14,0],[5,2],[13,2],[15,11],[15,6],[15,12],[4,6],[12,0],[6,14],[6,4],[11,4],[4,2],[7,4],[11,6],[7,12],[3,9],[2,11],[14,6],[2,1],[14,13],[9,15],[4,14],[6,3],[13,10],[8,10],[3,11],[4,3],[15,13],[12,10],[9,4],[3,6],[0,2],[12,9],[0,12],[15,11],[15,12],[6,11],[2,12],[4,7],[13,8],[1,0],[13,0],[8,4],[3,0],[9,12],[6,3],[12,3],[0,6],[7,5],[13,12],[15,5],[8,4],[10,15],[12,13],[9,12],[5,15],[9,3],[11,13],[5,15],[8,9],[2,12],[13,8],[13,2],[0,15],[10,11],[6,4],[9,10],[15,3],[15,11],[6,3],[7,9],[1,8],[7,0],[5,1],[9,1],[15,6],[5,3],[4,3],[11,3],[6,14],[0,10],[2,4],[15,11],[12,13],[5,8],[13,10],[12,5],[15,4],[2,11],[0,15],[4,2],[14,5],[7,15],[7,0],[6,12],[6,13],[5,14],[12,7],[3,4],[15,2],[2,4],[6,15],[13,15],[12,3],[14,7],[2,6],[15,14],[1,8],[2,13],[12,8],[12,1],[12,6],[0,5],[9,6],[3,7],[2,9],[5,12],[15,7],[15,2],[2,10],[3,5],[12,0],[7,1],[6,11],[12,0],[6,10],[4,12],[3,12],[9,14],[12,0],[6,0],[8,1],[12,11],[11,4],[7,12],[14,1],[1,14],[11,8],[1,4],[12,0],[5,15],[5,10],[11,10],[9,8],[5,6],[15,8],[12,0],[9,15],[0,6],[4,7],[14,5],[3,6],[4,8],[14,3],[0,1],[6,2],[13,2],[1,4],[8,6],[9,0],[13,6],[4,0],[11,1],[1,12],[0,10],[12,2],[7,14],[6,15],[5,15],[11,12],[12,0],[8,13],[2,7],[8,14],[10,12],[11,7],[4,1],[8,10],[8,7],[0,7],[7,11],[5,3],[10,12],[3,9],[4,2],[10,14],[14,11],[7,12],[5,12],[6,12],[14,11],[14,12]],[[6,7],[11,4],[6,9],[7,12],[7,15],[0,2],[13,3],[3,15],[8,6],[0,7],[2,11],[5,10],[15,3],[14,3],[12,8],[2,15],[9,3],[4,10],[12,6],[15,4],[0,5],[11,10],[1,12],[5,11],[8,13],[14,13],[3,2],[8,4],[14,4],[7,6],[11,6],[11,5],[3,15],[7,9],[4,1],[11,7],[15,14],[11,13],[3,12],[14,1],[1,9],[11,4],[13,15],[6,3],[1,6],[2,4],[6,1],[6,10],[4,0],[11,14],[15,14],[9,10],[8,10],[13,5],[2,4],[15,6],[7,6],[13,12],[0,14],[6,13],[1,6],[12,9],[10,4],[2,5],[0,15],[7,3],[3,4],[1,6],[7,11],[6,11],[8,0],[11,6],[9,15],[4,0],[12,14],[13,10],[12,1],[14,5],[13,6],[2,7],[6,11],[4,10],[11,0],[15,7],[12,14],[15,12],[9,7],[3,14],[8,9],[4,13],[4,11],[4,7],[13,9],[2,12],[12,15],[5,9],[10,0],[15,3],[8,10],[6,3],[3,7],[11,10],[14,7],[2,12],[9,11],[14,15],[10,1],[11,2],[6,3],[4,15],[11,0],[4,7],[1,7],[14,8],[6,0],[7,11],[14,6],[0,15],[4,2],[15,11],[0,14],[4,15],[11,4],[3,2],[8,13],[14,11],[10,12],[5,9],[10,7],[15,6],[7,12],[10,0],[14,8],[4,14],[10,8],[5,7],[8,6],[5,15],[11,0],[0,3],[6,13],[14,5],[1,14],[0,15],[2,5],[14,4],[0,10],[10,6],[5,1],[5,2],[7,11],[6,2],[10,3],[15,11],[15,9],[14,10],[8,3],[5,0],[13,4],[12,1],[6,12],[9,1],[1,7],[3,2],[8,4],[15,9],[0,6],[10,12],[12,13],[11,7],[10,0],[3,8],[10,9],[11,10],[11,13],[14,7],[11,12],[5,10],[5,6],[7,5],[10,9],[9,13],[2,6],[0,11],[11,13],[0,12],[1,2],[5,11],[3,1],[15,7],[12,8],[12,11],[10,6],[2,4],[2,1],[4,13],[3,1],[0,1],[1,15],[14,13],[8,9],[15,6],[4,15],[2,14],[10,7],[13,12],[2,1],[0,10],[3,5],[10,2],[6,5],[13,5],[4,2],[15,1],[14,13],[14,6],[12,10],[0,4],[5,14],[13,0],[3,15],[7,4],[11,14],[14,3],[5,10],[2,3],[8,15],[6,15],[6,2],[1,9],[6,13],[3,11],[3,14],[13,11],[10,8],[14,11],[7,0],[3,5],[7,11],[14,4],[3,13],[3,9],[14,2],[15,14],[0,9],[3,11],[6,0],[2,11],[15,8],[8,3],[6,7],[9,5],[7,13],[14,6],[4,1],[8,12]],[[15,11],[3,5],[8,12],[6,4],[2,6],[9,3],[14,2],[14,7],[4,8],[13,12],[1,10],[2,8],[11,4],[2,7],[10,3],[11,13],[7,6],[13,4],[13,14],[9,0],[9,6],[14,9],[14,3],[12,5],[8,0],[6,10],[2,1],[4,11],[4,6],[10,5],[7,11],[8,4],[3,5],[5,8],[11,0],[11,8],[7,2],[4,0],[10,3],[10,12],[6,10],[1,12],[4,11],[2,10],[11,4],[4,9],[10,15],[3,2],[10,12],[14,7],[1,7],[10,12],[6,4],[9,12],[8,4],[14,11],[8,13],[12,3],[4,9],[2,10],[3,11],[2,9],[11,15],[5,7],[10,11],[10,1],[15,9],[3,4],[15,4],[9,5],[1,8],[11,0],[8,12],[13,4],[1,5],[10,7],[2,8],[2,3],[1,10],[1,12],[14,1],[3,5],[8,7],[13,7],[1,14],[7,11],[3,14],[9,10],[1,13],[4,7],[7,11],[1,4],[10,3],[12,10],[14,6],[11,7],[4,2],[10,7],[14,11],[9,5],[12,6],[11,7],[7,4],[12,0],[5,6],[15,3],[10,11],[5,10],[5,8],[2,12],[6,13],[3,6],[8,0],[1,3],[5,7],[7,13],[12,6],[6,0],[8,2],[15,12],[9,13],[2,8],[2,3],[2,12],[14,12],[3,12],[5,0],[12,2],[3,1],[7,1],[5,3],[8,10],[2,6],[4,8],[13,9],[8,12],[7,4],[9,14],[14,2],[13,4],[6,1],[10,4],[2,1],[2,5],[10,8],[10,6],[15,3],[0,2],[6,1],[0,14],[4,13],[12,11],[11,14],[1,11],[14,12],[15,0],[10,0],[15,12],[5,1],[12,4],[0,14],[1,13],[5,0],[12,0],[4,5],[14,9],[7,6],[8,14],[13,10],[12,6],[7,13],[15,13],[5,1],[7,6],[0,5],[0,11],[8,13],[5,7],[2,10],[2,0],[4,3],[12,4],[14,2],[12,3],[12,1],[10,13],[3,9],[4,9],[4,13],[4,11],[9,10],[3,4],[3,12],[1,6],[8,6],[13,1],[7,4],[12,14],[6,10],[9,7],[0,7],[12,1],[8,12],[6,7],[15,13],[15,6],[10,14],[8,10],[8,2],[3,9],[12,6],[6,10],[2,4],[5,4],[3,1],[4,7],[15,14],[5,9],[11,1],[5,2],[3,8],[7,1],[12,4],[6,2],[7,12],[3,2],[15,10],[4,1],[2,4],[0,12],[5,4],[1,14],[11,4],[0,6],[14,8],[8,1],[9,4],[2,6],[3,1],[14,13],[4,6],[5,13],[5,15],[1,14],[6,9],[6,3],[3,6],[6,9],[5,0],[15,14],[13,15],[8,10],[7,1],[6,12],[3,14],[12,13]],[[3,11],[10,1],[2,5],[12,15],[4,5],[13,3],[3,13],[11,10],[6,5],[7,9],[5,12],[12,7],[14,15],[7,0],[2,0],[6,2],[14,6],[9,1],[15,13],[14,12],[10,6],[3,12],[7,9],[13,6],[10,3],[6,13],[15,9],[7,0],[4,1],[6,10],[7,15],[2,6],[13,6],[15,7],[12,1],[1,5],[8,7],[3,13],[15,5],[7,1],[8,2],[11,2],[12,5],[0,10],[10,9],[2,10],[13,1],[0,7],[11,0],[2,10],[8,11],[6,12],[4,2],[5,4],[14,9],[7,4],[6,14],[5,12],[4,11],[1,7],[12,13],[11,10],[5,1],[13,14],[15,7],[11,4],[4,2],[11,5],[8,3],[0,1],[11,13],[13,2],[7,15],[5,9],[14,8],[11,14],[12,14],[12,2],[6,12],[14,7],[3,11],[8,10],[14,0],[14,12],[12,0],[14,4],[9,14],[15,6],[9,1],[12,8],[2,14],[10,14],[9,1],[2,0],[13,5],[13,3],[12,10],[4,7],[8,9],[1,11],[2,6],[8,11],[12,3],[14,6],[1,2],[12,9],[0,6],[15,6],[0,12],[7,10],[9,4],[12,1],[4,0],[5,3],[10,3],[6,2],[4,6],[8,0],[12,2],[3,15],[13,6],[0,8],[10,8],[10,6],[11,12],[6,9],[2,5],[12,10],[3,7],[3,9],[14,10],[6,0],[8,14],[7,11],[8,15],[0,11],[0,6],[15,4],[10,3],[5,4],[1,8],[2,3],[1,10],[6,5],[1,11],[9,15],[11,12],[7,10],[9,11],[11,7],[10,4],[15,7],[9,14],[9,12],[8,4],[4,13],[13,6],[4,8],[4,8],[15,3],[3,13],[0,4],[1,14],[5,12],[12,9],[3,12],[4,11],[15,10],[0,2],[7,6],[14,4],[4,13],[13,10],[7,10],[0,2],[15,11],[10,8],[7,4],[10,2],[11,9],[14,9],[1,6],[10,8],[6,7],[7,1],[7,9],[13,4],[3,8],[14,3],[7,1],[1,4],[2,7],[12,15],[9,0],[2,14],[13,14],[5,2],[6,11],[0,4],[6,1],[3,4],[3,9],[6,13],[10,12],[0,15],[0,10],[9,15],[3,6],[3,12],[0,11],[4,0],[6,4],[12,0],[13,0],[0,2],[0,15],[15,8],[4,6],[6,0],[3,6],[15,9],[7,13],[12,4],[11,15],[15,7],[2,9],[11,1],[10,6],[9,8],[4,14],[6,12],[1,0],[9,4],[7,11],[12,15],[7,9],[8,2],[6,13],[12,14],[8,10],[15,12],[10,11],[11,5],[5,4],[9,1],[15,5],[0,13],[8,9],[9,7],[2,12],[9,4],[3,2],[0,8],[2,12],[9,7],[4,15]],[[0,8],[11,10],[13,3],[0,3],[2,1],[12,7],[8,3],[14,2],[8,11],[0,15],[0,5],[14,0],[3,14],[3,4],[2,15],[1,9],[14,13],[0,11],[9,3],[12,1],[9,3],[14,10],[14,13],[15,11],[1,0],[14,12],[2,6],[4,11],[6,8],[4,9],[13,5],[10,8],[10,9],[12,14],[7,11],[6,10],[11,12],[1,11],[0,2],[9,4],[13,10],[9,5],[2,5],[4,9],[7,13],[14,1],[15,4],[10,4],[2,11],[4,2],[4,15],[2,6],[6,7],[4,9],[5,10],[7,12],[11,4],[15,6],[10,6],[12,0],[10,11],[1,7],[0,12],[12,9],[11,5],[7,15],[6,14],[14,6],[12,7],[8,2],[1,11],[12,6],[10,11],[12,4],[7,4],[3,9],[2,12],[0,11],[9,0],[8,4],[8,15],[15,11],[2,12],[5,4],[14,7],[3,9],[0,9],[12,0],[0,7],[5,3],[3,12],[14,10],[11,15],[7,15],[1,6],[1,4],[0,7],[15,2],[2,15],[2,9],[0,14],[5,15],[12,15],[12,3],[5,3],[0,14],[15,5],[11,4],[0,9],[11,15],[15,1],[5,4],[1,12],[5,10],[15,7],[11,5],[5,11],[12,10],[5,15],[7,2],[4,6],[0,14],[11,2],[1,14],[15,10],[13,12],[1,0],[1,4],[11,8],[14,15],[9,5],[1,0],[2,4],[4,6],[8,10],[4,1],[15,7],[8,0],[3,7],[4,15],[1,13],[1,13],[11,0],[3,12],[15,7],[13,9],[7,14],[6,13],[4,2],[9,12],[0,14],[5,10],[5,11],[8,3],[7,15],[4,12],[7,6],[5,7],[13,3],[1,6],[12,9],[12,15],[0,11],[7,4],[8,7],[12,8],[11,14],[10,11],[11,7],[9,12],[10,12],[9,0],[1,8],[2,4],[0,8],[10,0],[13,5],[6,2],[12,7],[4,8],[8,15],[1,3],[4,5],[1,10],[9,4],[8,3],[10,11],[12,14],[4,8],[15,13],[8,9],[4,7],[8,1],[6,8],[12,4],[5,0],[9,13],[5,6],[8,4],[11,5],[10,5],[12,0],[0,10],[9,4],[3,13],[14,11],[11,12],[0,11],[10,14],[3,7],[12,14],[3,4],[12,2],[4,2],[11,3],[11,7],[15,14],[0,11],[10,8],[15,1],[7,13],[13,2],[4,7],[7,12],[2,15],[9,1],[15,12],[0,15],[11,12],[14,9],[0,3],[2,8],[11,15],[2,0],[11,2],[6,14],[4,14],[6,13],[9,14],[10,14],[9,13],[4,6],[2,11],[13,3],[1,5],[5,3],[8,5],[12,2],[6,0],[0,11],[0,7],[4,12],[11,3],[6,2],[8,12],[1,9]],[[3,14],[3,8],[6,10],[6,4],[7,14],[10,13],[0,15],[9,6],[4,8],[12,4],[13,6],[12,3],[11,12],[0,14],[1,15],[3,6],[0,13],[13,11],[4,13],[1,0],[4,0],[7,3],[2,1],[1,14],[14,10],[0,11],[15,5],[11,7],[8,1],[8,12],[6,8],[12,13],[10,14],[1,10],[15,10],[6,1],[14,5],[0,9],[6,2],[10,11],[6,14],[7,8],[8,2],[10,11],[4,12],[7,4],[5,2],[10,13],[6,14],[2,13],[0,9],[2,14],[6,5],[2,4],[3,0],[0,8],[11,7],[3,14],[1,14],[4,8],[2,14],[6,10],[9,0],[4,12],[10,7],[6,0],[7,5],[2,14],[8,11],[7,3],[3,10],[8,6],[13,12],[2,6],[4,3],[1,11],[1,14],[4,5],[5,7],[11,0],[4,5],[4,7],[13,15],[8,15],[3,5],[11,3],[2,14],[4,9],[12,6],[8,15],[0,6],[5,15],[10,11],[9,14],[6,2],[1,11],[12,6],[8,1],[1,2],[12,0],[13,3],[10,5],[6,8],[2,8],[1,0],[7,9],[13,3],[6,11],[7,6],[0,4],[15,11],[5,11],[8,10],[6,14],[8,14],[9,12],[5,13],[8,7],[15,10],[2,8],[15,0],[0,12],[5,11],[10,8],[3,5],[4,7],[9,10],[2,9],[0,2],[14,1],[3,4],[14,10],[2,14],[6,12],[4,8],[3,13],[12,7],[14,1],[5,12],[12,9],[12,9],[13,3],[5,4],[6,9],[6,11],[0,3],[6,9],[3,1],[13,0],[4,14],[14,0],[8,5],[4,10],[9,7],[6,1],[15,0],[4,12],[8,6],[14,9],[3,12],[8,9],[3,13],[14,10],[0,14],[2,3],[1,4],[6,0],[7,14],[12,7],[14,12],[4,13],[10,14],[13,11],[13,7],[5,4],[1,8],[0,4],[5,6],[1,6],[6,8],[11,9],[5,7],[5,4],[2,4],[2,9],[15,13],[7,0],[3,4],[8,1],[4,13],[6,5],[9,15],[12,4],[12,13],[7,1],[11,3],[2,15],[1,7],[13,7],[2,1],[7,1],[13,14],[5,4],[12,1],[15,3],[14,13],[4,9],[2,15],[11,15],[5,9],[12,9],[2,14],[9,3],[12,5],[7,11],[5,10],[7,8],[2,0],[3,2],[4,6],[15,13],[3,11],[1,15],[13,5],[15,0],[2,4],[7,15],[10,11],[5,2],[11,8],[14,12],[5,4],[2,12],[12,15],[13,3],[6,10],[2,15],[4,9],[10,7],[7,10],[14,6],[15,11],[15,13],[6,7],[9,1],[3,14],[9,1],[7,4],[11,1],[10,5],[15,0],[10,13],[6,14],[15,9],[2,15],[13,0]],[[13,11],[10,14],[5,10],[11,15],[5,3],[3,11],[0,5],[0,10],[5,14],[15,10],[4,13],[1,14],[3,7],[14,5],[3,10],[14,10],[0,15],[13,12],[13,3],[12,13],[0,5],[1,7],[9,10],[6,7],[12,10],[15,2],[6,9],[6,9],[9,15],[12,7],[0,6],[4,15],[5,11],[7,0],[8,6],[8,15],[10,13],[12,8],[8,4],[12,6],[10,15],[6,2],[15,0],[14,5],[10,0],[15,14],[4,13],[13,12],[11,7],[6,2],[8,13],[3,2],[7,0],[12,13],[1,9],[11,14],[0,8],[7,10],[11,13],[2,7],[3,4],[15,14],[1,5],[13,4],[0,10],[10,6],[6,15],[11,14],[14,7],[11,15],[8,13],[13,2],[1,3],[15,11],[0,3],[11,4],[0,6],[10,13],[15,3],[13,7],[10,12],[6,10],[9,5],[9,0],[5,13],[12,7],[4,0],[9,11],[4,5],[12,9],[0,8],[9,10],[13,7],[14,0],[3,7],[14,7],[4,5],[0,12],[9,2],[6,7],[0,9],[14,13],[9,11],[7,5],[1,13],[1,15],[9,4],[1,0],[10,6],[10,0],[3,13],[11,15],[8,13],[10,13],[12,13],[4,2],[0,8],[8,1],[1,6],[12,6],[1,11],[4,1],[11,3],[9,3],[12,5],[2,15],[0,14],[10,1],[11,4],[5,10],[9,13],[12,9],[15,5],[0,14],[11,1],[0,12],[13,8],[6,13],[3,11],[8,4],[0,15],[15,8],[8,1],[4,13],[11,0],[14,6],[12,0],[0,4],[2,7],[2,13],[8,0],[5,11],[7,1],[4,7],[14,3],[7,1],[4,12],[6,3],[11,8],[7,0],[15,11],[0,13],[12,9],[13,6],[1,12],[11,14],[4,5],[5,11],[0,1],[15,13],[13,5],[1,5],[12,15],[5,14],[9,8],[14,9],[15,12],[6,5],[3,0],[3,9],[13,12],[10,7],[13,7],[2,11],[10,1],[8,12],[3,14],[9,0],[2,9],[13,10],[6,14],[2,12],[8,2],[10,6],[14,12],[7,1],[9,15],[12,15],[10,6],[1,15],[6,13],[0,3],[9,2],[7,5],[15,1],[14,1],[9,4],[10,11],[14,10],[6,5],[3,10],[9,7],[9,5],[3,15],[7,4],[7,15],[1,7],[13,10],[9,11],[8,12],[1,5],[13,4],[11,9],[6,11],[7,13],[9,8],[15,10],[1,3],[3,12],[15,12],[0,8],[10,8],[9,2],[4,14],[0,14],[15,4],[1,10],[11,8],[1,15],[7,5],[11,0],[7,6],[15,3],[6,0],[12,4],[6,1],[8,14],[14,15],[1,9],[5,10],[15,11],[15,11],[11,9],[6,8],[0,2],[12,3]],[[4,8],[5,15],[5,8],[6,0],[2,13],[5,13],[11,14],[9,8],[13,0],[2,12],[11,6],[15,4],[13,5],[2,13],[3,15],[9,5],[1,12],[3,1],[4,9],[2,14],[15,2],[3,9],[3,0],[8,15],[6,14],[5,10],[12,15],[0,14],[14,1],[13,2],[10,13],[12,0],[12,8],[12,14],[1,9],[12,2],[15,11],[11,1],[12,4],[2,8],[15,2],[0,1],[15,1],[4,13],[4,0],[5,13],[4,0],[0,6],[15,1],[15,14],[14,5],[9,5],[3,11],[6,14],[4,3],[3,7],[8,1],[2,0],[14,13],[1,13],[1,4],[13,2],[15,3],[13,0],[3,14],[12,10],[3,10],[14,7],[11,15],[4,2],[14,10],[6,9],[13,3],[6,4],[4,8],[2,7],[13,1],[1,12],[9,6],[3,1],[13,8],[10,5],[7,2],[9,5],[4,1],[12,3],[9,1],[6,2],[10,2],[2,7],[2,7],[11,12],[4,1],[12,2],[6,3],[7,10],[2,10],[2,11],[1,11],[15,8],[15,10],[9,13],[3,4],[9,3],[12,10],[11,3],[15,4],[1,11],[5,6],[8,4],[8,12],[14,9],[0,5],[3,13],[12,8],[14,0],[1,8],[15,12],[7,3],[13,7],[1,12],[3,12],[4,11],[2,6],[13,15],[7,2],[1,13],[3,2],[1,8],[2,7],[3,6],[8,12],[3,5],[8,9],[13,14],[1,10],[15,7],[4,6],[13,3],[1,15],[13,7],[15,1],[0,2],[4,11],[0,10],[11,2],[13,3],[1,9],[15,14],[2,12],[10,11],[1,3],[8,3],[13,7],[7,0],[6,15],[0,7],[12,8],[3,5],[14,4],[2,6],[14,2],[3,11],[1,4],[1,0],[10,15],[11,10],[5,8],[1,11],[5,13],[7,10],[11,9],[0,1],[13,4],[10,9],[12,10],[10,0],[3,6],[2,14],[5,4],[0,12],[14,4],[5,8],[4,13],[13,5],[2,13],[1,6],[7,2],[13,7],[3,7],[1,14],[5,1],[13,5],[7,6],[4,9],[6,12],[12,1],[15,4],[14,13],[0,5],[4,6],[8,0],[2,7],[3,10],[12,11],[15,13],[9,15],[12,8],[8,15],[13,11],[10,12],[11,1],[11,3],[3,5],[7,10],[1,7],[5,11],[9,12],[13,15],[3,2],[1,5],[14,5],[9,11],[2,8],[8,9],[5,14],[15,8],[8,1],[3,9],[11,14],[7,2],[15,2],[9,8],[4,7],[8,5],[4,7],[6,9],[9,1],[3,1],[14,8],[12,7],[14,7],[9,0],[12,8],[2,11],[4,9],[11,10],[8,13],[6,9],[11,2],[5,8],[5,12],[2,14],[8,11],[5,0],[1,3]],[[5,13],[14,10],[15,13],[1,13],[12,0],[0,9],[3,13],[10,6],[12,3],[4,13],[5,6],[4,15],[15,13],[14,0],[0,7],[9,0],[8,3],[13,3],[4,7],[4,14],[0,3],[3,7],[0,15],[5,9],[8,7],[6,11],[10,4],[8,10],[13,8],[6,0],[12,7],[1,7],[14,4],[7,4],[10,13],[10,0],[15,5],[5,11],[6,13],[6,12],[14,5],[3,9],[11,5],[15,10],[8,7],[13,2],[8,11],[12,1],[2,5],[4,2],[5,4],[14,3],[11,4],[6,2],[14,1],[13,2],[8,10],[3,12],[15,0],[4,8],[13,11],[12,8],[3,7],[4,6],[7,10],[8,0],[1,9],[12,14],[6,3],[7,4],[10,13],[9,1],[2,13],[8,7],[11,3],[13,3],[14,8],[3,11],[7,11],[12,6],[10,14],[4,2],[5,12],[13,15],[3,15],[1,11],[1,0],[0,1],[9,4],[8,7],[13,12],[14,3],[15,13],[3,13],[1,2],[0,11],[1,13],[3,5],[4,7],[5,7],[7,2],[2,14],[3,11],[8,11],[15,2],[4,5],[4,15],[5,10],[15,11],[4,13],[8,4],[9,15],[5,13],[2,14],[8,0],[5,14],[11,8],[2,0],[12,8],[12,0],[13,15],[8,3],[12,3],[7,13],[8,13],[3,11],[0,10],[13,11],[4,10],[2,13],[9,11],[0,11],[1,2],[1,9],[14,2],[6,15],[4,5],[8,3],[12,1],[14,1],[12,3],[2,10],[7,2],[13,14],[12,3],[4,8],[0,1],[3,6],[2,11],[0,10],[14,0],[4,2],[2,14],[2,13],[11,8],[3,14],[8,13],[1,12],[7,3],[2,7],[4,9],[3,1],[15,2],[1,13],[6,10],[4,13],[1,4],[15,5],[9,2],[4,13],[10,7],[11,12],[13,3],[15,1],[3,7],[8,6],[9,15],[0,15],[6,9],[5,0],[6,3],[15,8],[9,4],[3,8],[11,0],[1,12],[8,0],[14,2],[5,1],[4,9],[15,2],[8,13],[3,4],[12,1],[11,12],[1,10],[8,14],[7,13],[15,9],[11,8],[5,12],[10,11],[12,5],[11,12],[15,4],[2,12],[15,4],[8,6],[9,8],[14,6],[8,5],[4,2],[10,11],[11,9],[2,10],[15,11],[11,5],[11,3],[12,5],[8,4],[13,11],[8,10],[14,0],[13,2],[5,6],[6,3],[5,14],[2,6],[12,2],[6,14],[5,4],[11,8],[12,15],[9,5],[4,11],[13,9],[14,11],[4,9],[13,9],[5,15],[12,3],[15,14],[13,4],[15,2],[1,2],[9,8],[4,7],[12,4],[15,4],[10,6],[11,7],[5,12],[9,8],[11,10],[6,13],[4,5]],[[4,8],[15,1],[3,14],[5,4],[0,4],[6,8],[11,7],[1,12],[10,6],[8,6],[4,0],[15,11],[12,9],[1,7],[3,2],[8,4],[6,3],[15,6],[0,6],[3,11],[5,12],[8,11],[0,7],[4,3],[7,6],[3,14],[11,3],[11,12],[5,11],[8,14],[5,0],[0,10],[2,4],[4,8],[2,8],[5,1],[2,14],[7,11],[3,13],[8,13],[7,15],[1,9],[5,1],[6,11],[2,15],[14,1],[7,4],[5,1],[2,5],[12,6],[1,4],[5,8],[4,13],[13,0],[9,12],[5,2],[15,10],[2,8],[13,1],[10,5],[0,12],[6,1],[12,4],[7,2],[3,6],[10,7],[0,9],[8,6],[12,2],[0,10],[9,10],[11,4],[9,3],[6,11],[10,15],[0,3],[4,1],[14,12],[11,0],[4,5],[5,15],[7,9],[1,4],[11,8],[14,15],[3,1],[4,9],[14,10],[13,6],[3,10],[2,13],[3,10],[1,7],[14,13],[4,10],[14,0],[2,1],[3,8],[3,0],[9,14],[5,0],[3,14],[0,1],[11,9],[13,6],[0,6],[11,1],[13,11],[5,2],[9,15],[15,2],[14,0],[10,2],[10,1],[2,1],[12,5],[4,12],[14,3],[3,2],[12,5],[1,10],[0,1],[9,6],[12,5],[6,11],[7,10],[7,12],[8,1],[11,7],[4,1],[9,10],[9,7],[3,15],[12,4],[3,7],[6,5],[11,13],[5,14],[2,13],[10,14],[8,14],[6,2],[3,10],[7,4],[4,9],[14,5],[1,13],[3,13],[7,4],[1,13],[15,6],[15,4],[11,10],[13,2],[8,0],[1,8],[4,5],[5,7],[4,14],[3,5],[1,0],[5,14],[9,5],[5,9],[5,1],[4,1],[1,12],[8,4],[0,8],[12,3],[11,9],[13,11],[11,13],[0,4],[9,8],[4,14],[2,11],[8,9],[13,12],[15,6],[9,7],[0,11],[12,0],[5,12],[4,1],[4,14],[13,7],[0,12],[8,9],[15,12],[14,12],[2,6],[7,9],[14,2],[1,9],[13,6],[14,8],[6,3],[8,12],[11,9],[11,1],[5,10],[12,3],[11,1],[8,14],[15,7],[8,9],[0,11],[12,13],[15,2],[12,9],[10,13],[2,11],[10,3],[4,14],[0,11],[7,12],[3,9],[1,15],[2,6],[0,9],[15,4],[5,15],[0,11],[13,2],[11,9],[14,6],[9,15],[10,15],[11,2],[5,12],[14,12],[9,14],[12,14],[15,12],[0,13],[11,15],[15,9],[8,1],[3,10],[5,7],[7,13],[12,13],[1,13],[10,5],[10,14],[9,11],[3,12],[14,15],[9,3],[9,11],[8,0],[10,7],[9,3],[6,13],[3,7]],[[3,8],[5,13],[15,11],[12,8],[6,4],[15,14],[14,5],[2,7],[6,5],[4,14],[10,8],[8,5],[5,6],[5,4],[6,15],[1,13],[14,8],[0,2],[0,9],[14,6],[6,13],[13,11],[9,6],[9,11],[5,6],[6,7],[3,14],[10,6],[1,10],[8,15],[8,4],[10,11],[10,8],[13,9],[6,1],[2,10],[9,3],[4,5],[4,0],[9,10],[15,7],[8,10],[11,15],[2,3],[13,6],[10,8],[10,8],[10,13],[7,11],[8,12],[2,15],[2,10],[7,6],[8,5],[4,14],[8,0],[6,4],[3,4],[9,10],[10,4],[7,11],[5,11],[4,1],[10,9],[13,1],[10,14],[14,2],[11,2],[7,15],[1,9],[11,3],[13,9],[15,13],[13,1],[2,8],[11,9],[6,5],[0,4],[8,2],[4,10],[0,15],[8,6],[10,14],[12,6],[7,9],[0,14],[2,8],[4,10],[11,9],[4,11],[12,14],[15,12],[7,9],[4,7],[2,8],[10,13],[4,6],[10,13],[15,11],[5,10],[9,8],[11,7],[4,9],[4,7],[2,6],[12,15],[4,13],[8,7],[11,9],[14,3],[15,1],[12,9],[9,1],[13,1],[3,15],[1,7],[3,1],[13,4],[13,12],[5,12],[6,14],[5,12],[4,15],[11,7],[4,11],[11,7],[8,6],[12,13],[12,11],[13,14],[6,10],[8,13],[0,12],[9,6],[2,5],[13,6],[1,8],[13,8],[13,2],[1,5],[0,2],[4,7],[9,1],[7,14],[3,6],[5,8],[1,5],[12,4],[5,15],[4,1],[10,9],[1,9],[10,15],[3,5],[11,15],[7,8],[6,4],[3,8],[11,13],[15,6],[0,6],[0,14],[9,13],[4,2],[12,10],[3,10],[5,12],[11,9],[12,2],[2,15],[10,6],[12,8],[3,12],[8,10],[4,10],[15,7],[8,1],[10,5],[15,3],[15,14],[10,6],[8,3],[5,15],[8,11],[13,11],[12,4],[10,0],[1,6],[7,8],[0,11],[3,11],[0,4],[6,4],[0,9],[0,14],[6,12],[7,1],[15,12],[14,13],[1,13],[2,4],[5,15],[11,15],[0,8],[9,8],[15,14],[15,14],[0,6],[11,1],[3,7],[12,11],[5,13],[14,5],[15,0],[6,11],[2,12],[13,0],[6,14],[8,6],[6,15],[8,14],[7,6],[10,12],[2,0],[2,9],[0,8],[0,7],[9,13],[15,8],[11,6],[13,3],[2,8],[7,11],[3,6],[6,7],[4,0],[14,15],[8,2],[0,12],[13,6],[6,5],[6,0],[11,5],[4,12],[8,10],[5,11],[4,14],[1,13],[11,12],[15,6],[6,14],[1,2],[1,3],[1,13],[14,5],[15,2]],[[1,3],[7,15],[5,0],[7,14],[3,0],[9,7],[3,10],[1,13],[1,5],[6,13],[6,4],[3,2],[12,8],[14,3],[5,1],[3,6],[0,9],[3,4],[0,13],[0,6],[6,2],[11,6],[1,0],[7,13],[15,11],[7,11],[10,15],[5,1],[12,5],[13,8],[2,11],[1,4],[1,2],[0,11],[9,8],[0,5],[14,7],[1,7],[10,12],[11,15],[15,3],[15,13],[1,11],[1,9],[8,10],[12,2],[5,6],[4,11],[12,0],[14,5],[11,0],[6,11],[15,13],[0,8],[6,5],[6,11],[3,0],[4,14],[6,10],[1,6],[13,14],[13,4],[10,12],[6,0],[13,4],[3,7],[15,11],[2,14],[10,1],[5,12],[5,11],[15,0],[10,8],[13,10],[0,2],[5,2],[7,10],[10,3],[13,12],[3,5],[4,6],[0,9],[5,0],[8,11],[2,13],[9,11],[13,14],[11,6],[10,8],[15,7],[12,11],[12,9],[1,3],[10,0],[1,4],[4,11],[0,1],[7,0],[11,14],[0,4],[6,9],[5,9],[5,0],[3,6],[3,7],[11,13],[4,15],[0,2],[3,13],[10,12],[2,9],[4,5],[9,4],[9,1],[4,12],[1,0],[15,9],[12,13],[11,12],[6,11],[5,9],[11,15],[5,7],[0,4],[15,0],[9,11],[3,2],[10,6],[12,14],[11,4],[6,14],[15,6],[2,15],[5,4],[13,12],[2,1],[2,14],[12,0],[4,12],[10,5],[10,4],[15,12],[3,14],[12,14],[5,7],[7,8],[2,5],[3,7],[1,8],[9,0],[5,0],[11,8],[14,3],[5,8],[5,0],[12,6],[2,5],[7,9],[13,9],[8,12],[11,14],[11,7],[8,13],[5,11],[7,3],[10,1],[10,5],[9,11],[15,3],[9,13],[4,7],[0,8],[8,12],[1,7],[5,13],[5,6],[14,6],[5,14],[15,5],[13,14],[11,3],[6,10],[13,11],[11,0],[11,0],[12,15],[3,8],[1,11],[4,1],[8,10],[7,10],[2,14],[15,1],[6,12],[5,8],[12,6],[11,9],[14,15],[2,12],[0,11],[0,11],[10,8],[11,1],[9,11],[9,13],[0,4],[10,13],[15,0],[2,11],[14,9],[13,9],[9,7],[10,13],[5,9],[11,0],[8,4],[13,11],[3,4],[3,5],[7,14],[4,5],[10,12],[0,6],[6,5],[9,6],[2,3],[13,15],[13,0],[0,12],[5,14],[15,14],[4,5],[12,6],[15,6],[0,1],[15,12],[4,13],[2,1],[13,10],[2,15],[3,10],[14,2],[14,9],[12,9],[0,7],[0,6],[14,13],[8,2],[3,6],[14,7],[1,14],[3,12],[11,5],[12,5],[14,3],[5,1]],[[12,14],[11,6],[14,11],[7,5],[13,8],[6,0],[3,14],[4,10],[6,8],[5,0],[1,12],[3,15],[3,1],[8,7],[5,2],[0,4],[10,13],[3,7],[0,10],[8,11],[10,6],[3,8],[5,12],[11,10],[5,4],[8,7],[8,3],[14,12],[9,12],[12,14],[8,2],[1,5],[3,13],[6,14],[13,11],[2,5],[6,3],[3,9],[4,0],[4,10],[11,0],[0,15],[11,8],[4,7],[1,8],[8,7],[12,10],[4,2],[8,6],[4,0],[10,1],[10,0],[15,10],[9,14],[5,6],[1,0],[3,11],[11,13],[2,7],[8,11],[7,4],[9,6],[14,13],[13,11],[13,2],[2,6],[6,1],[12,8],[7,5],[0,9],[3,13],[14,5],[9,14],[5,8],[6,3],[12,9],[15,1],[11,2],[2,6],[4,9],[9,14],[8,11],[7,0],[5,13],[5,0],[3,15],[12,3],[9,15],[8,11],[11,15],[6,8],[7,6],[1,7],[3,15],[1,0],[1,2],[9,0],[2,14],[5,6],[0,5],[10,12],[3,12],[14,15],[14,13],[7,13],[11,4],[0,15],[2,7],[8,2],[4,8],[7,5],[12,15],[8,13],[9,12],[11,5],[13,8],[9,0],[15,9],[15,6],[1,11],[7,3],[5,11],[4,15],[5,1],[7,0],[13,11],[0,11],[7,2],[4,15],[7,13],[1,15],[11,6],[5,2],[4,12],[5,12],[7,10],[11,0],[2,5],[4,5],[7,1],[1,8],[4,7],[7,11],[15,6],[9,4],[4,12],[12,0],[8,14],[2,11],[0,2],[9,1],[7,12],[6,12],[12,3],[2,9],[11,3],[0,9],[1,13],[2,8],[4,2],[9,3],[0,8],[11,9],[5,8],[11,0],[9,2],[0,13],[10,0],[10,1],[7,12],[5,2],[12,0],[5,13],[5,2],[13,6],[7,8],[2,1],[3,15],[1,7],[8,12],[5,4],[3,15],[3,10],[11,9],[2,9],[14,9],[5,10],[0,5],[1,9],[4,11],[2,14],[8,7],[13,2],[9,12],[12,13],[5,4],[0,1],[7,2],[14,7],[2,9],[12,9],[4,0],[5,14],[14,11],[11,7],[15,9],[3,1],[15,5],[11,14],[1,13],[10,2],[15,3],[3,11],[2,13],[7,6],[8,3],[2,11],[6,0],[3,11],[15,9],[10,12],[1,8],[4,0],[4,0],[15,3],[2,10],[6,10],[9,12],[1,15],[2,11],[2,12],[7,12],[15,6],[0,5],[4,15],[9,10],[1,11],[0,8],[9,8],[9,2],[0,4],[0,1],[9,8],[14,0],[11,14],[14,0],[1,4],[0,5],[9,5],[4,11],[15,6],[2,11],[10,5],[3,4],[7,4],[2,7]],[[14,7],[2,8],[5,0],[5,10],[9,12],[14,4],[14,10],[14,12],[9,5],[15,0],[5,2],[3,12],[2,6],[12,1],[9,15],[3,11],[7,8],[1,4],[5,11],[6,13],[9,7],[9,11],[13,3],[10,12],[7,2],[13,0],[4,8],[2,9],[0,11],[7,5],[8,2],[5,9],[9,2],[8,15],[8,11],[15,0],[0,12],[0,9],[4,3],[8,12],[0,9],[7,14],[8,7],[5,12],[8,5],[13,0],[14,0],[1,0],[9,2],[0,6],[15,13],[13,3],[7,11],[1,8],[11,1],[8,13],[14,3],[0,7],[13,1],[14,0],[4,10],[10,8],[6,7],[7,10],[1,7],[15,14],[5,15],[10,6],[3,15],[2,12],[8,3],[11,9],[1,15],[5,14],[14,9],[4,5],[8,9],[1,2],[11,0],[2,0],[2,5],[3,8],[13,2],[2,0],[13,4],[2,7],[5,8],[9,15],[13,10],[5,6],[4,1],[6,9],[7,4],[10,12],[0,6],[3,12],[14,4],[6,15],[15,12],[3,8],[2,7],[1,0],[15,14],[10,4],[3,13],[5,6],[14,4],[0,7],[8,2],[5,9],[8,2],[9,14],[6,3],[9,6],[0,15],[1,3],[10,5],[0,7],[8,9],[5,8],[3,10],[1,6],[13,11],[5,15],[5,7],[15,2],[15,8],[14,10],[1,12],[10,3],[9,1],[4,3],[12,6],[11,8],[7,13],[7,0],[11,10],[5,3],[14,11],[8,1],[8,10],[3,6],[7,15],[2,9],[11,5],[4,5],[6,7],[7,10],[14,4],[12,14],[6,2],[8,14],[11,3],[1,5],[12,7],[4,6],[9,1],[0,11],[12,11],[10,7],[11,15],[0,7],[13,5],[5,8],[6,2],[14,11],[14,13],[0,15],[14,6],[9,4],[2,13],[9,10],[13,12],[10,8],[8,7],[15,10],[4,0],[13,12],[3,11],[12,10],[3,6],[3,9],[12,11],[1,13],[13,1],[7,5],[6,5],[10,6],[0,3],[15,7],[7,6],[4,9],[9,1],[12,13],[2,10],[3,11],[6,3],[3,7],[0,5],[4,1],[10,15],[5,0],[11,10],[4,2],[1,3],[6,8],[3,11],[7,3],[0,4],[9,10],[13,12],[15,7],[0,7],[10,14],[12,8],[13,10],[0,15],[2,15],[12,6],[7,15],[12,7],[5,6],[14,8],[15,8],[5,12],[15,9],[7,0],[5,8],[3,10],[10,7],[11,1],[14,5],[2,11],[15,14],[1,0],[11,1],[3,9],[8,1],[10,13],[1,7],[12,14],[12,2],[2,9],[11,4],[14,9],[4,1],[11,5],[10,9],[14,15],[4,1],[2,15],[2,15],[0,7],[10,4],[11,13],[4,6]],[[3,7],[12,4],[1,15],[15,5],[7,10],[10,3],[11,6],[3,9],[7,13],[11,6],[15,3],[5,12],[0,15],[12,1],[4,6],[1,8],[4,11],[13,8],[2,4],[14,12],[3,15],[13,6],[5,7],[1,10],[7,13],[1,15],[1,15],[4,7],[1,13],[4,3],[9,7],[8,10],[3,4],[6,10],[0,14],[10,5],[8,3],[9,7],[2,14],[3,2],[7,6],[3,11],[2,3],[8,2],[10,2],[5,8],[10,9],[9,7],[3,1],[2,11],[13,2],[3,8],[10,8],[8,6],[15,3],[14,15],[13,8],[2,13],[9,12],[10,0],[9,7],[2,0],[2,11],[6,8],[8,9],[7,1],[11,10],[9,1],[11,14],[0,6],[3,13],[2,13],[2,11],[12,4],[13,12],[13,7],[9,0],[15,4],[10,8],[13,8],[3,7],[13,11],[6,11],[8,3],[5,15],[5,6],[14,7],[4,6],[7,13],[9,5],[3,7],[0,9],[13,3],[14,4],[10,5],[6,7],[13,3],[4,11],[8,10],[2,14],[13,12],[0,5],[11,14],[2,7],[12,0],[6,0],[15,14],[6,15],[11,7],[4,11],[12,7],[14,1],[5,15],[8,5],[13,2],[7,12],[1,6],[8,14],[2,12],[0,9],[7,4],[2,9],[11,7],[14,12],[6,5],[8,11],[8,10],[12,2],[6,11],[3,12],[8,6],[2,5],[1,8],[1,12],[15,14],[2,15],[14,11],[11,10],[3,0],[0,5],[0,5],[12,9],[8,1],[9,3],[6,1],[1,4],[1,11],[9,4],[6,0],[10,11],[7,10],[11,10],[5,13],[3,4],[8,13],[1,3],[4,5],[7,12],[3,6],[14,3],[15,0],[4,9],[5,15],[2,8],[10,14],[1,2],[0,12],[7,13],[0,10],[10,5],[7,14],[11,13],[3,8],[9,11],[4,10],[5,12],[12,11],[9,6],[5,0],[1,0],[13,2],[14,3],[10,11],[5,10],[5,7],[7,12],[9,13],[5,15],[14,9],[3,13],[3,8],[12,3],[7,10],[10,3],[6,0],[7,2],[12,10],[9,8],[11,12],[14,1],[3,1],[6,1],[1,4],[6,12],[6,4],[15,4],[7,10],[2,1],[0,7],[2,9],[13,4],[14,13],[2,15],[15,11],[4,5],[10,1],[9,13],[8,5],[5,11],[10,9],[1,7],[4,15],[7,13],[11,5],[13,15],[3,6],[0,2],[10,11],[9,5],[13,5],[6,5],[10,8],[14,5],[12,6],[2,6],[1,6],[3,2],[10,2],[5,8],[11,4],[2,7],[0,8],[7,0],[13,6],[6,14],[0,2],[15,7],[0,9],[11,4],[12,4],[2,1],[1,4],[8,13],[0,1],[10,11],[9,14]]]
YW = 574
def setup_inputs(rng):
    return {"x": rng.standard_normal((N, 128, T), dtype=np.float32)}
def reference(x):
    y = np.full((N, 128, YW), np.nan, x.dtype)
    fill = [0] * N
    for r in range(N):
        for t in range(T):
            for e in ROUTE[r][t]:
                y[e][:, fill[e]] = x[r][:, t]
                fill[e] += 1
    return {"y": y}

from concourse.bass import DstId, RemoteDMATransfer

SCRATCH = {
    "xs": ("sbuf", [128, 256], "float32"),
    "land": ("sbuf", [128, 574], "float32"),
    "pk": ("sbuf", [128, 48], "float32"),
}
SEMAPHORES = ["xin", "pg0", "pg1", "ph0", "ph1", "sent", "arrived", "stored"]

ON_CHIP, OFF_CHIP = 0xFFFF, 0x00FF
_CACHE = {}


def _runs(route_s, d):
    out = []
    for t, pair in enumerate(route_s):
        if d in pair:
            if out and out[-1][0] + out[-1][1] == t:
                out[-1] = (out[-1][0], out[-1][1] + 1)
            else:
                out.append((t, 1))
    return out


def _plan(route, cores, topo):
    if "plan" in _CACHE:
        return _CACHE["plan"]
    n = len(route)
    runs = [[_runs(route[s], d) for d in range(n)] for s in range(n)]
    cnt = [[sum(ln for _, ln in runs[s][d]) for d in range(n)] for s in range(n)]
    off = [[sum(cnt[r][d] for r in range(s)) for d in range(n)] for s in range(n)]
    chip = [c // 8 for c in cores]

    def crosses(s, d):
        return chip[s] % 2 != chip[d] % 2

    def work(s, d):
        return len(runs[s][d]) + 1

    def loads(s, d):
        if crosses(s, d):
            out = [("mate", chip[s], cnt[s][d])]
            if chip[d] != chip[s] ^ 1:
                out += [("switch", ("out", chip[s] ^ 1), cnt[s][d]), ("switch", ("in", chip[d]), cnt[s][d])]
        else:
            out = [("switch", ("out", chip[s]), cnt[s][d]), ("switch", ("in", chip[d]), cnt[s][d])]
        return out + [("work", (s, crosses(s, d)), work(s, d))]

    seats = {}
    for s in range(n):
        for h in range(8):
            c = cores[s] - 5 + h
            seats.setdefault((s, topo.may_write(c, c ^ 8), topo.die(c)), []).append(h)
    home_die = [topo.die(c) for c in cores]
    extra = [len(runs[s][s]) + 9 for s in range(n)]

    die = [[None] * n for _ in range(n)]
    groups = []
    load = {}
    for s in range(n):
        load[("work", (s, False), home_die[s])] = extra[s]
        for far in (False, True):
            grp = [d for d in range(n) if d != s and crosses(s, d) == far]
            free = [2 * len(seats[(s, far, k)]) for k in (0, 1)]
            if not far:
                free[home_die[s]] -= 1
            k = 1 - home_die[s]
            for d in grp:
                if not free[k]:
                    k = 1 - k
                if not free[k]:
                    raise ValueError("more blocks than seats")
                die[s][d] = k
                free[k] -= 1
                for kind, place, w in loads(s, d):
                    load[(kind, place, k)] = load.get((kind, place, k), 0) + w
                    load.setdefault((kind, place, 1 - k), 0)
                k = 1 - k
            groups.append((s, grp))

    fair = {}
    for kind, place, k in load:
        fair[kind] = max(fair.get(kind, 0), (load[(kind, place, 0)] + load[(kind, place, 1)]) / 2.0)

    for power in (2, 4, 8, 16, 32):
        better = True
        while better:
            better = False
            for s, grp in groups:
                for a in grp:
                    for b in grp:
                        if die[s][a] == 1 and die[s][b] == 0:
                            change = {}
                            for d in (a, b):
                                k = die[s][d]
                                for kind, place, w in loads(s, d):
                                    change[(kind, place, k)] = change.get((kind, place, k), 0) - w
                                    change[(kind, place, 1 - k)] = change.get((kind, place, 1 - k), 0) + w
                            gain = sum(((load[key] + dv) / fair[key[0]]) ** power - (load[key] / fair[key[0]]) ** power
                                       for key, dv in change.items())
                            if gain < -1e-9:
                                for key, dv in change.items():
                                    load[key] += dv
                                die[s][a], die[s][b] = 0, 1
                                better = True

    blocks = {}
    for s, grp in groups:
        far = crosses(s, grp[0])
        for k in (0, 1):
            mine = [d for d in grp if die[s][d] == k]
            c0, c1 = seats[(s, far, k)]
            base = [extra[s] if h == 5 else 0 for h in (c0, c1)]
            room = [1 if h == 5 else 2 for h in (c0, c1)]
            best = None
            for bits in range(1 << len(mine)):
                part = [[d for i, d in enumerate(mine) if (bits >> i) & 1 == j] for j in (0, 1)]
                if len(part[0]) <= room[0] and len(part[1]) <= room[1]:
                    top = max(base[j] + sum(work(s, d) for d in part[j]) for j in (0, 1))
                    if best is None or top < best[0]:
                        best = (top, part)
            for j, h in enumerate((c0, c1)):
                blocks[(s, h)] = sorted(best[1][j], key=lambda d: (d - s) % n) + ([s] if h == 5 else [])
    _CACHE["plan"] = (runs, cnt, off, blocks)
    return _CACHE["plan"]


def rank_program(g, core, T, topo):
    home = core - core % 8 + 5
    s = T.rank_of(home)
    if s is None:
        return
    runs, cnt, off, blocks = _plan(T.tables["ROUTE"], T.cores, topo)
    n = len(cnt)
    sem = T.sem
    is_rank = core == home
    left = 0

    if is_rank:
        g.sync.dma_start(T.xs[:], T.x[:]).then_inc(sem.xin, 16)
    for q in (g, g.sync, g.scalar):
        q.wait_ge(sem.xin, 16)

    if is_rank:
        ids = []
        for h in range(8):
            if home - 5 + h != core:
                rid, pid = topo.addr(home - 5 + h, core)
                ids.append(DstId(rid=rid, pnc=pid))
        g.remote_dma_fused([RemoteDMATransfer(dst_ids=ids, dma_engine_mask=ON_CHIP, remote_sem=sem.xin,
                                              srcs=[T.xs[:]], dsts=[T.xs[:]] * len(ids))], local_sem=sem.sent)
        left += 16

    stage = T.pk if is_rank else T.land
    queues = (g, g.sync, g.scalar)
    packed = []
    turn = 0
    base = 0
    for b, d in enumerate(blocks[(s, core % 8)]):
        buf, at = (T.land, off[s][s]) if d == s else (stage, base)
        if at + cnt[s][d] > buf.shape[1]:
            raise ValueError("block does not fit its buffer")
        issued = [0, 0]
        pos = at
        for t, ln in runs[s][d]:
            mine = turn % 3 == 0
            queues[turn % 3].dma_start(buf[:, pos:pos + ln], T.xs[:, t:t + ln]).then_inc(
                sem[("pg%d" if mine else "ph%d") % b], 16)
            issued[0 if mine else 1] += 16
            pos += ln
            turn += 1
        packed.append((b, d, at, issued))
        if d != s:
            base += cnt[s][d]

    for b, d, at, issued in packed:
        if issued[0]:
            g.wait_ge(sem["pg%d" % b], issued[0])
        if issued[1]:
            g.wait_ge(sem["ph%d" % b], issued[1])
        if d != s and cnt[s][d]:
            rid, pid = topo.addr(T.cores[d], core)
            g.remote_dma(T.land[:, off[s][d]:off[s][d] + cnt[s][d]], stage[:, at:at + cnt[s][d]],
                         sem.arrived, sem.sent, pid, rid, OFF_CHIP)
            left += 8
    if left:
        g.wait_ge(sem.sent, left)

    if is_rank:
        g.wait_ge(sem.arrived, 8 * sum(1 for r in range(n) if r != s and cnt[r][s]))
        total = sum(cnt[r][s] for r in range(n))
        g.dma_start(T.y[:, 0:total], T.land[:, 0:total]).then_inc(sem.stored, 16)
        g.wait_ge(sem.stored, 16)
